import numpy as np, ml_dtypes
CORES = [25,29,65,69,153,157,193,197]
N = 8
BF = ml_dtypes.bfloat16
def f(rng, *shape):
    return (rng.standard_normal(shape, dtype=np.float32) * np.exp2(rng.integers(-2, 3, shape[:-1] + (1,)))).astype(BF)
def wide(rng, *shape):
    v = f(rng, *shape).astype(np.float32); k = shape[:-2] + (1, shape[-1])
    return (v * np.exp2(rng.integers(-6, 7, k)) * (rng.random(k) > 0.0625)).astype(BF)
def gentries(a):
    return np.ascontiguousarray(a.reshape(8, 16, -1).transpose(0, 2, 1)).reshape(8, -1)
def gtable(e):
    e = np.asarray(e); return np.ascontiguousarray(e.reshape(8, -1, 16).transpose(0, 2, 1)).reshape(128, -1).astype(np.int32)
E, S, D, F, R, V = 1024, 192, 48, 6, 3, 16384
W = E + (N - 1) * S
def arrive(a, snd):
    out = []
    for r in range(N):
        part = [a[r]]
        for t in range(1, N):
            q = (r + t) % N; p = gentries(snd[q]).reshape(8, N - 1, S)[:, N - 1 - t]
            part.append(np.take_along_axis(a[q], p[:, None, :], axis=2))
        out.append(np.concatenate(part, axis=2))
    return np.stack(out)
def slots(rng, lo, hi):
    return np.stack([rng.permuted(np.tile(np.arange(lo, hi), (8 * (N - 1), 1)), axis=1)[:, :S].reshape(8, N - 1, S) for r in range(N)])
def preds(rng):
    v = np.where(rng.random((N, 8, F, E)) < 0.5, rng.integers(0, E, (N, 8, F, E)), rng.integers(E, W, (N, 8, F, E)))
    v[:, :, 1] = np.where(rng.random((N, 8, E)) < 0.0625, v[:, :, 0], v[:, :, 1]); return v
def nodes(rng):
    return rng.integers(0, V, (N, 8, E))
def codes(rng):
    return rng.integers(0, D, (N, 8, E))
def make(rng, v, p, s, c):
    snd = np.stack([gtable(p[r].reshape(8, -1)) for r in range(N)]); a = arrive(s[:, :, None, :], snd)
    sf = np.take_along_axis(a, v.reshape(N, 8, 1, F * E), axis=3).reshape(N, 8, F, E)
    d = np.take_along_axis(sf, rng.integers(0, F, (N, 8, 1, E)), axis=2)[:, :, 0]; u = rng.integers(0, 8, (N, 8, E))
    d = np.where(u < 5, d, np.where(u < 7, d ^ 1, rng.integers(0, V, (N, 8, E))))
    return {"x": f(rng, N, 128, E), "tab": (rng.random((N, 128, D * D), dtype=np.float32) * 2 - 1).astype(BF), "dirs": c.astype(np.int32), "srcs": s.astype(np.int32), "dsts": d.astype(np.int32),
            "nb": np.stack([gtable(v[r].reshape(8, -1)) for r in range(N)]), "snd": snd}
def setup_inputs(rng):
    return make(rng, preds(rng), slots(rng, 0, E), nodes(rng), codes(rng))
def setup_inputs_ends(rng):
    p = slots(rng, 1, E - 1); p[..., 0] = E - 1; p[..., S - 1] = 0
    v = np.where(rng.random((N, 8, F, E)) < 0.75, rng.choice(np.array([0, 1, E - 1, E, E + S - 1, E + S, W - S, W - 1]), (N, 8, F, E)), preds(rng))
    return make(rng, v, p, rng.choice(np.array([0, 1, V - 2, V - 1]), (N, 8, E)), rng.choice(np.array([0, 1, D - 2, D - 1]), (N, 8, E)))
def setup_inputs_back(rng):
    s = 2 * rng.integers(0, V // 2, (1, 8, 1)) + rng.integers(0, 2, (N, 8, E))
    return make(rng, preds(rng), slots(rng, 0, E), s, codes(rng))
def setup_inputs_far(rng):
    v = rng.integers(E, W, (N, 8, F, E)); a = rng.permutation(N); t = int(rng.integers(0, N - 1))
    v[a[0]] = E + t * S + rng.integers(0, S, (8, F, E)); v[a[1]] = rng.integers(0, E, (8, F, E))
    p = slots(rng, 0, E); p[:] = p[:, :, :1].copy()
    return make(rng, v, p, nodes(rng), codes(rng))
def setup_inputs_alike(rng):
    v = preds(rng); v[:] = v[:, :, :1].copy()
    c = np.broadcast_to(rng.integers(0, D, (N, 8, 1)), (N, 8, E))
    return make(rng, v, slots(rng, 0, E), nodes(rng), c)
def setup_inputs_spread(rng):
    d = setup_inputs(rng); d["x"] = wide(rng, N, 128, E); return d
def check_inputs(d):
    bad = []
    for name, top in (("nb", W), ("snd", E), ("dirs", D), ("srcs", V), ("dsts", V)):
        if not ((d[name] >= 0) & (d[name] < top)).all(): bad.append(name + " in its range")
    p = np.stack([gentries(d["snd"][r]).reshape(8 * (N - 1), S) for r in range(N)])
    if not (np.diff(np.sort(p, axis=2), axis=2) > 0).all(): bad.append("different edges in the slots of a pair and group")
    if not (np.abs(d["x"].astype(np.float64)) <= 2.0 ** 40).all(): bad.append("x finite and at most 2**40 in size")
    if not (np.abs(d["tab"].astype(np.float64)) <= 1).all(): bad.append("tab at most 1 in size")
    return bad
def reference(x, tab, dirs, srcs, dsts, nb, snd):
    xs = x.astype(np.float64).reshape(N, 8, 16, E); v = np.stack([gentries(nb[r]) for r in range(N)])
    df = np.take_along_axis(arrive(dirs[:, :, None, :], snd)[:, :, 0], v, axis=2)
    sf = np.take_along_axis(arrive(srcs[:, :, None, :], snd)[:, :, 0], v, axis=2)
    off = D * df + np.tile(dirs, (1, 1, F)); back = sf == np.tile(dsts, (1, 1, F))
    w = []
    for r in range(N):
        c = np.take_along_axis(tab[r].astype(np.float64).reshape(8, 16, D * D), off[r][:, None, :], axis=2)
        w.append(np.where(back[r][:, None, :], 0.0, c * 0.25))
    m = xs
    for k in range(R):
        a = arrive(m, snd); new = []
        for r in range(N):
            term = w[r] * np.take_along_axis(a[r], v[r][:, None, :], axis=2)
            new.append(np.maximum(xs[r] + np.sum(term.reshape(8, 16, F, E), axis=2), 0.0))
        m = np.stack(new)
    return {"y": m.reshape(N, 128, E).astype(np.float32)}

from concourse.bass import DstId, RemoteDMATransfer
from concourse.mybir import AluOpType as Op, ActivationFunctionType as Act

E, S, H, W, DD, SIM = 1024, 192, 96, 2368, 2304, 256

SCRATCH = {
    "iw": ("sbuf", [128, E], "int32"), "sn": ("sbuf", [128, 7, 12], "int32"), "sns": ("sbuf", [128, 7, 12], "int32"),
    "nbi": ("sbuf", [128, 384], "int32"), "nbs": ("sbuf", [128, 192], "int32"),
    "snu": ("sbuf", [128, 84], "uint16"), "sl": ("sbuf", [128, 84], "uint16"), "nbu": ("sbuf", [128, 384], "uint16"),
    "ml": ("sbuf", [128, 384], "uint16"), "ol": ("sbuf", [128, 384], "uint16"),
    "pc": ("sbuf", [128, 4], "int32"), "cf": ("sbuf", [128, 16], "float32"), "jj": ("sbuf", [128, 256], "float32"),
    "s1f": ("sbuf", [128, 208], "bfloat16"), "s2f": ("sbuf", [128, 208], "bfloat16"),
    "s1e": ("sbuf", [128, 208], "bfloat16"), "s2e": ("sbuf", [128, 208], "bfloat16"),
    "pm": ("sbuf", [128, 128], "float32"), "idm": ("sbuf", [128, 128], "float32"),
    "xm": ("sbuf", [128, 128], "bfloat16"), "js": ("sbuf", [128, 128], "float32"),
    "xw": ("sbuf", [128, W], "bfloat16"), "mw": ("sbuf", [128, W], "bfloat16"),
    "out0": ("sbuf", [128, 7 * S], "bfloat16"), "out1": ("sbuf", [128, 7 * S], "bfloat16"),
    "out2": ("sbuf", [128, 7 * H], "float32"), "out3": ("sbuf", [128, 7 * H], "float32"),
    "out4": ("sbuf", [128, 7 * H], "float32"), "out5": ("sbuf", [128, 7 * H], "float32"),
    "win0": ("sbuf", [128, W], "bfloat16"), "win1": ("sbuf", [128, W], "bfloat16"),
    "win2": ("sbuf", [128, W], "float32"), "win3": ("sbuf", [128, W], "float32"),
    "win4": ("sbuf", [128, W], "float32"), "win5": ("sbuf", [128, W], "float32"),
    "kg": ("sbuf", [128, 6 * E], "bfloat16"), "et": ("sbuf", [128, 256], "float32"),
    "aq": ("sbuf", [128, 384], "float32"), "at": ("sbuf", [128, 384], "float32"), "am": ("sbuf", [128, 384], "float32"),
    "mq": ("sbuf", [128, 192], "int32"), "md": ("sbuf", [128, 192], "float32"), "mg": ("sbuf", [128, 192], "float32"),
    "tab0": ("sbuf", [128, DD + 16], "bfloat16"), "tab1": ("sbuf", [128, DD + 16], "bfloat16"),
    "w0": ("sbuf", [128, 3 * E], "bfloat16"), "w1": ("sbuf", [128, 3 * E], "bfloat16"),
    "pr0": ("sbuf", [128, 3 * E], "float32"), "pr1": ("sbuf", [128, 3 * E], "float32"),
    "rg": ("sbuf", [128, 512], "float32"), "ys": ("sbuf", [128, 2 * E], "float32"),
    "acc0": ("psum", [128, 512], "float32"), "acc1": ("psum", [128, 512], "float32"),
    "acc2": ("psum", [128, 512], "float32"), "acc3": ("psum", [128, 512], "float32"),
    "pw0": ("psum", [128, 512], "float32"), "pw1": ("psum", [128, 512], "float32"),
    "pw2": ("psum", [128, 512], "float32"), "pe0": ("psum", [128, 512], "float32"),
}
SEMAPHORES = (["cv", "cs", "ct", "cg", "lsn", "lrow", "lx", "lnb", "lsw", "ltab0", "ltab1", "lw0", "lw1", "st", "snt0", "snt1", "rs"]
              + ["rl%d" % k for k in range(6)] + ["ac0", "ac1"] + ["ad%d" % k for k in range(2, 6)]
              + ["af%d_%d" % (k, t) for k in range(2, 6) for t in range(7)])


def bits(engines):
    m = 0
    for e in engines:
        m |= 1 << e
    return m


def routes(T, topo):
    cores, via, used = list(T.cores), {}, set()
    for q, a in enumerate(cores):
        for r, b in enumerate(cores):
            if q == r or topo.may_write(a, b):
                continue
            if topo.die(a) == topo.die(b):
                pool = [c for c in range(SIM) if topo.mates(c, b)]
            else:
                pool = topo.cores_of(a)
            pool = [c for c in pool if topo.die(c) == topo.die(a) and topo.may_write(a, c) and topo.may_write(c, b)
                    and c not in used and T.rank_of(c) is None]
            via[(q, r)] = pool[0]
            used.add(pool[0])
    return via


def landing(T, k, q, r):
    t = (q - r) % len(T.cores) - 1
    if k == 0:
        return T.xw[:, E + t * S:E + (t + 1) * S]
    if k == 1:
        return T.mw[:, E + t * S:E + (t + 1) * S]
    return T["win%d" % k][:, E + t * S:E + t * S + H]


def relay_program(g, core, T, topo, q, r):
    b = T.cores[r]
    rid, pid = topo.addr(b, core)
    n = len(topo.engines(core, b))
    for k in range(6):
        wd = S if k < 2 else H
        sem = "ac%d" % k if k < 2 else "af%d_%d" % (k, (q - r) % len(T.cores) - 1)
        g.wait_ge(T.sem["rl%d" % k], n // 2)
        g.remote_dma(landing(T, k, q, r), T["out%d" % k][:, 0:wd], T.sem[sem], T.sem.rs, pid, rid, topo.mask(core, b))
    g.wait_ge(T.sem.rs, 6 * n)


def runs(ts):
    out = []
    for t in sorted(ts):
        if out and out[-1][1] == t:
            out[-1][1] = t + 1
        else:
            out.append([t, t + 1])
    return out


def rank_program(g, core, T, topo):
    via = routes(T, topo)
    rank = T.rank_of(core)
    if rank is None:
        for (q, r), c in via.items():
            if c == core:
                relay_program(g, core, T, topo, q, r)
        return
    N = len(T.cores)
    Q = {"v": g.vector, "s": g.scalar, "t": g.tensor, "g": g, "y": g.sync}
    cnt = {"v": 0, "s": 0, "t": 0, "g": 0}
    seen = {}

    def wait(e, *toks):
        for tok in toks:
            if seen.get((e, tok[0]), 0) < tok[1]:
                Q[e].wait_ge(T.sem[tok[0]], tok[1])
                seen[(e, tok[0])] = tok[1]

    def done(e, ins):
        cnt[e] += 1
        ins.then_inc(T.sem["c" + e], 1)
        return ("c" + e, cnt[e])

    def ts(out, in0, s1, s2, o0, o1, *deps):
        wait("v", *deps)
        if o1 is None:
            return done("v", g.vector.tensor_scalar(out, in0, s1, None, o0))
        return done("v", g.vector.tensor_scalar(out, in0, s1, s2, o0, o1))

    def tt(out, a, b, o, *deps):
        wait("v", *deps)
        return done("v", g.vector.tensor_tensor(out, a, b, o))

    def cp(out, a, *deps):
        wait("v", *deps)
        return done("v", g.vector.tensor_copy(out, a))

    def act(out, a, f, *deps):
        wait("s", *deps)
        return done("s", g.scalar.activation(out, a, f))

    def dma(e, out, a, sem):
        Q[e].dma_start(out, a).then_inc(T.sem[sem], 16)

    LO, UP = slice(0, 64), slice(64, 128)
    HALF = (LO, UP)

    far = [t for t in range(N - 1) if (rank, (rank + t + 1) % N) in via]
    near = [t for t in range(N - 1) if t not in far]
    hand = {t: via[((rank + t + 1) % N, rank)] for t in range(N - 1) if ((rank + t + 1) % N, rank) in via}
    far_in = sorted(hand, key=lambda t: topo.mates(hand[t], core))
    near_in = [t for t in range(N - 1) if t not in hand]

    def send(k, which):
        wd = S if k < 2 else H
        jobs = []
        for t in which:
            r = (rank + t + 1) % N
            src = T["out%d" % k][:, t * wd:(t + 1) * wd]
            if (rank, r) in via:
                jobs.append((via[(rank, r)], src, T["out%d" % k][:, 0:wd], "rl%d" % k))
            else:
                jobs.append((T.cores[r], src, landing(T, k, rank, r), ("ac%d" if k < 2 else "ad%d") % k))
        own = topo.cores_of(core)
        off = [j for j in jobs if j[0] not in own]
        on = [j for j in jobs if j[0] in own]
        eoff = topo.engines(core, off[0][0])
        eon = [e for e in topo.engines(core, on[0][0]) if e not in eoff]
        trs = []
        for lst, eng in ((off, eoff), (on, eon)):
            n = len(eng) // len(lst)
            for i, (c, src, dst, sem) in enumerate(lst):
                rid, pid = topo.addr(c, core)
                trs.append(RemoteDMATransfer(dst_ids=[DstId(rid=rid, pnc=pid)], dma_engine_mask=bits(eng[i * n:(i + 1) * n]),
                                             remote_sem=T.sem[sem], src=src, dst=dst))
        g.remote_dma_fused(trs, local_sem=T.sem["snt0" if k < 2 else "snt1"])

    n_hand = {t: len(topo.engines(hand[t], core)) for t in hand}
    n_call = len(topo.engines(core, [c for c in topo.cores_of(core) if c != core][0]))
    n_all = n_call + sum(n_hand.values())

    t_ms = done("v", g.vector.memset(T.iw[:], 0))
    dma("y", T.sn[:], T.snd[:], "lsn")
    dma("s", T.xw[:, 0:E], T.x[:], "lx")
    wait("y", t_ms)
    wait("s", t_ms)
    dma("y", T.iw[0:128:16, :], T.dirs[:], "lrow")
    dma("s", T.iw[2:128:16, :], T.dsts[:], "lrow")
    dma("y", T.iw[1:128:16, :], T.srcs[:], "lrow")
    dma("s", T.iw[4:128:16, :], T.dsts[:], "lrow")
    dma("y", T.iw[3:128:16, :], T.srcs[:], "lrow")
    dma("y", T.nbi[:], T.nb[:], "lnb")
    dma("y", T.nbs[LO, :], T.nb[UP, 192:384], "lsw")
    dma("y", T.nbs[UP, :], T.nb[LO, 192:384], "lsw")
    dma("y", T.sns[LO], T.snd[UP, :], "lsw")
    dma("y", T.sns[UP], T.snd[LO, :], "lsw")
    for h in HALF:
        dma("y", T.tab0[h, 0:DD], T.tab[LO, :], "ltab0")

    t_p = done("g", g.iota(T.pc[:, 0:1], [[1, 1]], 0, 1))
    t_j = done("g", g.iota(T.jj[:], [[0, 2], [1, 128]], 0, 0, allow_small_or_imprecise_dtypes=True))

    def col(i):
        return T.cf[:, i:i + 1]
    t_r = ts(T.pc[:, 1:2], T.pc[:, 0:1], 15, None, Op.bitwise_and, None, t_p)
    t_gq = ts(T.pc[:, 2:3], T.pc[:, 0:1], 112, None, Op.bitwise_and, None, t_p)
    t_a = ts(col(0), T.pc[:, 1:2], 3.0, 1.0 / 128, Op.is_lt, Op.max, t_r)
    t_b = ts(col(1), T.pc[:, 1:2], 3.0, -0.496, Op.is_ge, Op.mult, t_r)
    t_snu = cp(T.snu[:], T.sn[:], ("lsn", 16))
    t_c = [ts(col(2), T.pc[:, 2:3], 15.0, None, Op.add, None, t_gq),
           cp(col(3), T.pc[:, 0:1], t_p),
           ts(col(4), T.pc[:, 1:2], 0.0, 48.0 / 4096, Op.is_equal, Op.mult, t_r),
           ts(col(5), T.pc[:, 1:2], 0.0, 1.0 / 4096, Op.is_equal, Op.mult, t_r),
           ts(col(6), T.pc[:, 1:2], 1.0, None, Op.is_equal, None, t_r),
           ts(col(7), T.pc[:, 1:2], 3.0, 128.0, Op.is_equal, Op.mult, t_r),
           ts(col(8), T.pc[:, 1:2], 2.0, None, Op.is_equal, None, t_r),
           ts(col(9), T.pc[:, 1:2], 4.0, 128.0, Op.is_equal, Op.mult, t_r)]
    t_z = [done("v", g.vector.memset(T["tab%d" % b][:, DD:DD + 16], 0.0)) for b in range(2)]
    t_c.append(tt(col(6), col(6), col(7), Op.add, t_c[-1]))
    t_c.append(tt(col(8), col(8), col(9), Op.add, t_c[-1]))

    for which in (far, near):
        for a, b in runs(which):
            tok = act(T.out0[:, a * S:b * S], T.xw[:, 0:E].indirect(T.snu[:, a * 12:b * 12]), Act.Copy, ("lx", 16), t_snu)
        wait("g", tok)
        send(0, which)
    t1 = ts(T.iw[:], T.iw[:], col(0), col(1), Op.mult, Op.add, ("lrow", 80), t_a, t_b)
    t2 = ts(T.iw[:], T.iw[:], 127, None, Op.bitwise_and, None, t1)
    for which in (far, near):
        for a, b in runs(which):
            tok = cp(T.out1[:, a * S:b * S], T.iw[:, 0:E].indirect(T.snu[:, a * 12:b * 12]), t2, t_snu)
        wait("g", tok)
        send(1, which)

    wait("y", ("snt0", 4 * n_call))
    for b in range(2):
        for h in HALF:
            dma("y", T["win%d" % b][h, 0:E], T.x[HALF[b], :], "lw%d" % b)
    wait("y", ("ac0", n_all))
    for h in HALF:
        dma("y", T.win0[h, E:W], T.xw[LO, E:W], "lw0")
    for h in HALF:
        dma("y", T.tab1[h, 0:DD], T.tab[UP, :], "ltab1")
    for h in HALF:
        dma("y", T.win1[h, E:W], T.xw[UP, E:W], "lw1")

    t_own = cp(T.mw[:, 0:E], T.iw[:], t2)
    t_sel = {}
    for name, c in (("s1e", 5), ("s2e", 8), ("s1f", 4), ("s2f", 6)):
        t_sel[name] = ts(T[name][:], T.jj[:, 0:208], col(2), col(c), Op.is_equal, Op.mult, t_j, t_c[-1])
    t_nbu = cp(T.nbu[:], T.nbi[:], ("lnb", 16))

    def wrap(bank, src, base, names, *deps):
        wait("t", *deps)
        for o, name in enumerate(names):
            for p in range(2):
                for i in range(16):
                    s0 = 15 - i + 64 * p
                    ins = g.tensor.matmul(bank[:, o * 128 + p * 64:o * 128 + p * 64 + 64], T[name][:, s0:s0 + 128],
                                          src[:, base[p] + i:base[p] + E:16], i == 0, i == 15)
        return done("t", ins)

    t_e = wrap(T.pe0, T.mw, (0, 0), ("s1e", "s2e"), t_own, t_sel["s1e"], t_sel["s2e"])
    t_pm = ts(T.pm[:], T.jj[:, 64:192], col(3), None, Op.is_equal, None, t_c[-1])
    t_id = ts(T.idm[:], T.jj[:, 0:128], col(3), None, Op.is_equal, None)
    t_xm = tt(T.xm[:], T.pm[:], T.idm[:], Op.add, t_pm, t_id)
    t_js = ts(T.js[:], T.xm[:], 0.25, None, Op.mult, None, t_xm)
    cp(T.ml[LO, 0:192], T.nbu[LO, 0:192], t_nbu)
    cp(T.ml[UP, 192:384], T.nbu[UP, 0:192])
    cp(T.ml[UP, 0:192], T.nbs[UP, :], ("lsw", 64))
    t_ml = cp(T.ml[LO, 192:384], T.nbs[LO, :])
    cp(T.sl[LO, 0:42], T.sn[LO, :, 0:6])
    cp(T.sl[UP, 42:84], T.sn[UP, :, 0:6])
    cp(T.sl[UP, 0:42], T.sns[UP, :, 6:12])
    t_sl = cp(T.sl[LO, 42:84], T.sns[LO, :, 6:12])
    t_et = cp(T.et[:], T.pe0[:, 0:256], t_e)
    wait("t", t_xm, t_js, ("lx", 16))
    for eh in range(2):
        g.tensor.matmul(T["acc%d" % eh][:], T.xm[LO, :], T.xw[LO, eh * 512:eh * 512 + 512], True, False)

    t_meta = ("ac1", n_all)

    def key(e, c, a, b):
        o, i = T.kg[:, c * E + a:c * E + b], T.mw[:, 0:W].indirect(T.nbu[:, c * 64 + a // 16:c * 64 + b // 16])
        if e == "v":
            return cp(o, i, t_meta, t_own, t_nbu)
        return act(o, i, Act.Copy, t_meta, t_own, t_nbu)

    def offsets(c, t_w):
        bank, s = T["pw%d" % c], slice(c * 128, c * 128 + 128)
        t_q = tt(T.aq[:, s], bank[:, 128:256], T.et[:, 128:256], Op.is_equal, t_w, t_et)
        t_t = tt(T.at[:, s], bank[:, 0:128], T.et[:, 0:128], Op.add)
        t_m = tt(T.am[:, s], T.aq[:, s], T.at[:, s], Op.max, t_q, t_t)
        c0 = c * 128
        ts(T.ol[LO, s], T.am[LO, s], 4096.0, float(DD), Op.mult, Op.min, t_m)
        ts(T.ol[UP, c0:c0 + 64], T.am[UP, c0 + 64:c0 + 128], 4096.0, float(DD), Op.mult, Op.min)
        return ts(T.ol[UP, c0 + 64:c0 + 128], T.am[UP, c0:c0 + 64], 4096.0, float(DD), Op.mult, Op.min)

    def weights(b, c, eh):
        o = c * 128 + b * 64 + eh * 32
        return act(T["w%d" % b][:, c * E + eh * 512:c * E + eh * 512 + 512], T["tab%d" % b][:, 0:DD + 16].indirect(T.ol[:, o:o + 32]),
                   Act.Copy, t_ol[c], ("ltab%d" % b, 32), t_z[b])

    def ship(k, tok):
        b = k % 2
        for which in (far, near):
            for a, z in runs(which):
                t = act(T["out%d" % k][:, a * H:z * H], T["win%d" % k][:, 0:E].indirect(T.sl[:, b * 42 + a * 6:b * 42 + z * 6]),
                        Act.Copy, tok, t_sl)
            wait("g", t)
            send(k, which)

    sel = ("s1f", "s2f")
    t_ol = {}
    kv0, ks0 = key("v", 0, 0, E), key("s", 3, 0, E)
    w_0 = wrap(T.pw0, T.kg, (0, 3 * E), sel, kv0, ks0, t_sel["s1f"], t_sel["s2f"])
    kv1, ks1 = key("v", 1, 0, E), key("s", 4, 0, E)
    w_1 = wrap(T.pw1, T.kg, (E, 4 * E), sel, kv1, ks1)
    t_ol[0] = offsets(0, w_0)
    kv2 = key("v", 2, 0, 512)
    key("s", 5, 0, E)
    ks2 = key("s", 2, 512, E)
    w_2 = wrap(T.pw2, T.kg, (2 * E, 5 * E), sel, kv2, ks2)
    t_ol[1] = offsets(1, w_1)

    QW = E // 4
    t_rel, busy = {}, {}
    wps = (T.pe0, T.pw2)

    def batch(k, ready, between):
        b = k % 2
        pr, win, t_w = T["pr%d" % b], T["win%d" % k], {}
        if k >= 2:
            o = b * 192 + 160
            t_rg = act(T.rg[:], win[:, 0:W].indirect(T.ml[:, o:o + 32]), Act.Copy, *ready)
        else:
            for i in range(6):
                between(i)
                t_w[i] = weights(b, i % 3, i // 3)
        for q in range(4):
            name = "acc%d" % ((2 * b + q) % 4)
            acc = T[name][:, 0:QW]
            wait("t", busy.get(name, t_xm))
            g.tensor.matmul(acc, T.xm[HALF[b], :], T.xw[HALF[b], q * QW:q * QW + QW], True, False)
            shared = k >= 2 and q >= 2
            nc = 2 if shared else 3
            if shared:
                u = slice((q - 2) * QW, (q - 1) * QW)
                t_m = tt(T.pw0[:, u], T.rg[:, u], wps[b][:, u], Op.mult, t_rg, busy["pw0"])
            for c in range(nc):
                o, s = b * 192 + c * 64 + q * 16, slice(c * E + q * QW, c * E + q * QW + QW)
                tok = tt(pr[:, s], win[:, 0:W].indirect(T.ml[:, o:o + 16]), T["w%d" % b][:, s], Op.mult,
                         t_w.get(q // 2 * 3 + c, ready[0]), *ready)
                if shared and c == 0:
                    tok = busy["pw0"] = tt(pr[:, s], pr[:, s], T.pw0[:, u], Op.add, tok, t_m)
                wait("t", tok)
                t_mm = done("t", g.tensor.matmul(acc, T.js[:], pr[:, s], False, c == nc - 1))
            if k < 4:
                o = T["win%d" % (k + 2)][:, q * QW:q * QW + QW]
            else:
                o = T.ys[:, b * E + q * QW:b * E + q * QW + QW]
            busy[name] = t_rel[b] = act(o, acc, Act.Relu, t_mm)
            if k >= 4 and q % 2 == 1:
                wait("y", t_rel[b])
                dma("y", T.y[HALF[b], (q - 1) * QW:(q + 1) * QW], T.ys[LO, b * E + (q - 1) * QW:b * E + (q + 1) * QW], "st")
        return tok

    t_sum = {}
    for c in range(3):
        for eh in range(2):
            o, s = c * 64 + eh * 32, slice(c * E + eh * 512, c * E + eh * 512 + 512)
            tok = tt(T.pr0[:, s], T.win0[:, 0:W].indirect(T.ml[:, o:o + 32]), T.w0[:, s], Op.mult, weights(0, c, eh), t_ml, ("lw0", 64))
            wait("t", tok)
            t_sum[eh] = done("t", g.tensor.matmul(T["acc%d" % eh][:], T.js[:], T.pr0[:, s], False, c == 2))
            if (c, eh) == (0, 0):
                t_ol[2] = offsets(2, w_2)

    def finish_a(i):
        if i == 4:
            for eh in range(2):
                busy["acc%d" % eh] = t_rel[0] = act(T.win2[:, eh * 512:eh * 512 + 512], T["acc%d" % eh][:], Act.Relu, t_sum[eh])
            ship(2, t_rel[0])
    t_pr = batch(1, (t_ml, ("lw1", 64)), finish_a)
    ship(3, t_rel[1])

    m1 = ts(T.mq[:], T.nbs[:], 1.0 / H, -(E - 0.5) / H - 0.5, Op.mult, Op.add)
    m4 = ts(T.mg[:], T.nbs[:], float(E), None, Op.is_ge, None)
    m2 = ts(T.mq[:], T.mq[:], 1, None, Op.bitwise_and, None, m1)
    m3 = ts(T.md[:], T.mq[:], -float(S), float(H), Op.mult, Op.add, m2)
    m5 = tt(T.md[:], T.md[:], T.mg[:], Op.mult, m3, m4)
    m6 = tt(T.md[:], T.md[:], T.nbs[:], Op.add, m5)
    cp(T.ml[UP, 0:192], T.md[UP, :], m6, t_pr)
    t_ml = cp(T.ml[LO, 192:384], T.md[LO, :])

    for b in range(2):
        t_wp = cp(wps[b][:], T["w%d" % b][:, 2 * E + 512:3 * E], t_et, t_ol[2])
    busy["pw0"], busy["pw1"] = t_ol[0], t_ol[1]

    for k in range(2, 6):
        b = k % 2
        banks = ["pw0", "pw1", "acc%d" % (2 - 2 * b), "acc%d" % (3 - 2 * b)]
        came = [(t, ("ad%d" % k, n_call)) for t in near_in] + [(t, ("af%d_%d" % (k, t), n_hand[t])) for t in far_in]
        for j, (t, arrived) in enumerate(came):
            name, c0 = banks[(j + 3) % 4], E + t * S
            wait("t", arrived, busy[name], t_pm)
            tm = done("t", g.tensor.matmul(T[name][:, 0:H], T.pm[:], T["win%d" % k][:, c0:c0 + H], True, True))
            busy[name] = t_win = cp(T["win%d" % k][:, c0 + H:c0 + S], T[name][:, 0:H], tm)
        batch(k, (t_win, t_ml, t_wp, t_rel[b]), None)
        if k < 4:
            ship(k + 2, t_rel[b])

    wait("g", ("snt1", 8 * n_call))
    wait("y", ("cv", cnt["v"]), ("ct", cnt["t"]), ("cs", cnt["s"]), ("cg", cnt["g"]), ("st", 64))
